import numpy as np
import ml_dtypes


def mxq(x, axis, fmt="e4m3"):
    dtype, down = {"e4m3": (ml_dtypes.float8_e4m3fn, 7), "e5m2": (ml_dtypes.float8_e5m2, 14)}[fmt]
    v = np.moveaxis(np.asarray(x, np.float32).astype(ml_dtypes.bfloat16).astype(np.float64), axis, -1)
    blocks = v.reshape(v.shape[:-1] + (-1, 32))
    amax = np.abs(blocks).max(-1, keepdims=True)
    byte = np.maximum(np.where(amax > 0, np.frexp(amax)[1] - 1 + 127, 0) - down, 1)
    scale = np.exp2(byte - 127.0)
    codes = (blocks / scale).astype(np.float32).astype(dtype).astype(np.float64)
    return np.moveaxis((codes * scale).reshape(v.shape), -1, axis)


WIDE = False


def mx_kscale(k):
    if not WIDE:
        return np.ones(k)
    levels = np.array([30, -30])
    if k % 512:
        return np.exp2(np.random.permutation(np.resize(levels, k // 32))).repeat(32)
    a = np.empty((k // 512, 16))
    for p in range(k // 512):
        a[p, :8] = np.random.permutation(np.resize(levels, 8))
        for g in range(8):
            far = levels[np.abs(levels - a[p, g]) >= 10]
            a[p, g + 8] = far[np.random.randint(len(far))]
    return np.exp2(a.ravel()).repeat(32)


def f64(x):
    return np.asarray(x).astype(np.float64)


def striped(idx):
    return np.tile(np.asarray(idx).reshape(-1, 16).T, (8, 1)).astype(np.uint16)


def unstriped(offs):
    return offs[:16].T.reshape(-1).astype(np.int64)


E2M1 = np.array([0.0, 0.5, 1.0, 1.5, 2.0, 3.0, 4.0, 6.0, -0.0, -0.5, -1.0, -1.5, -2.0, -3.0, -4.0, -6.0])


def pack_weight(w, fmt):
    k, n = w.shape
    w = f64(np.asarray(w, np.float32).astype(ml_dtypes.bfloat16)).reshape(k // 32, 32, n)
    amax = np.abs(w).max(1)
    if fmt in ("e4m3", "e5m2"):
        byte = np.frexp(amax)[1] - 1 + 127 - (7 if fmt == "e4m3" else 14)
    else:
        mant, ex = np.frexp(amax / 6.0)
        byte = np.where(mant > 0.5, ex, ex - 1) + 127
    byte = np.clip(np.where(amax > 0, byte, 1), 1, 254)
    scaled = (w * np.exp2(127.0 - byte)[:, None, :]).reshape(k, n).astype(np.float32)
    by_word = np.ascontiguousarray(scaled.reshape(k // 512, 128, 4, n).transpose(0, 1, 3, 2))
    if fmt in ("e4m3", "e5m2"):
        words = by_word.astype(ml_dtypes.float8_e4m3fn if fmt == "e4m3" else ml_dtypes.float8_e5m2).view(np.uint8)
    else:
        c = by_word.astype(ml_dtypes.float4_e2m1fn).view(np.uint8) & 0xF
        words = (c[..., 0::2] | (c[..., 1::2] << 4)).reshape(k // 512, 128, 2 * n)
    return np.ascontiguousarray(words), np.ascontiguousarray(byte.astype(np.uint8).reshape(k // 512, 16, n))


def unpack_weight(words, scales, fmt):
    g, _, n = scales.shape
    words = np.ascontiguousarray(words).reshape(g, 128, n, -1)
    if fmt in ("e4m3", "e5m2"):
        vals = words.view(ml_dtypes.float8_e4m3fn if fmt == "e4m3" else ml_dtypes.float8_e5m2).astype(np.float64)
    else:
        nib = np.empty((g, 128, n, 4), np.uint8)
        nib[..., 0::2] = words & 0xF
        nib[..., 1::2] = words >> 4
        vals = E2M1[nib]
    vals = vals * np.repeat(np.exp2(scales.astype(np.float64) - 127.0), 8, axis=1)[..., None]
    return vals.transpose(0, 1, 3, 2).reshape(g * 512, n)


K, T, J, R, V, N, Z, E = 512, 2048, 256, 512, 512, 256, 1024, 128


def setup_inputs():
    n = np.random.standard_normal
    idx = np.random.permutation(T)[:J]
    idx2 = np.random.permutation(Z)[:J]
    idx3 = np.random.permutation(V)[:J]
    idx4 = np.random.permutation(V)[:J]
    idx5 = np.random.permutation(J)[:E]
    idx6 = np.random.permutation(J)[:E]
    fk = mx_kscale(K)
    fr = mx_kscale(R)
    xtp = pack_weight(n((K, T)) / fk[:, None], "e5m2")
    wp = pack_weight(n((K, R)) * 1 / np.sqrt(K) * fk[:, None] * fr, "e2m1")
    xop = pack_weight(n((K, Z)) / fk[:, None], "e4m3")
    wbp = pack_weight(n((R, N)) * 1 / np.sqrt(R) / fr[:, None], "e2m1")
    return {
        "xt_words": xtp[0],
        "xt_scales": xtp[1],
        "w_words": wp[0],
        "w_scales": wp[1],
        "xo_words": xop[0],
        "xo_scales": xop[1],
        "tb": (n((R, V))).astype(np.float32),
        "wb_words": wbp[0],
        "wb_scales": wbp[1],
        "offs": striped(idx),
        "offs2": striped(idx2),
        "offs3": striped(idx3),
        "offs4": striped(idx4),
        "offs5": striped(idx5),
        "offs6": striped(idx6),
    }


def reference(xt_words, xt_scales, w_words, w_scales, xo_words, xo_scales, tb, wb_words, wb_scales, offs, offs2, offs3, offs4, offs5, offs6):
    idx = unstriped(offs)
    idx2 = unstriped(offs2)
    idx3 = unstriped(offs3)
    idx4 = unstriped(offs4)
    idx5 = unstriped(offs5)
    idx6 = unstriped(offs6)
    xtu = unpack_weight(xt_words, xt_scales, "e5m2")
    wu = unpack_weight(w_words, w_scales, "e2m1")
    xou = unpack_weight(xo_words, xo_scales, "e4m3")
    wbu = unpack_weight(wb_words, wb_scales, "e2m1")
    xtidxg = xtu[:, idx]
    a = wu.T @ xtidxg
    xoidx2g = xou[:, idx2]
    da = wu.T @ xoidx2g
    hid = a * f64(tb)[:, idx3]
    dh = da * f64(tb)[:, idx3] + a * f64(tb)[:, idx4]
    hidq = mxq(hid, 0, "e4m3")
    p = wbu.T @ hidq
    dhq = mxq(dh, 0, "e5m2")
    dp = wbu.T @ dhq
    y = p[:, idx5] - 0.5 * dp[:, idx6]
    return y

@@ -1,0 +1,192 @@
+from contextlib import ExitStack
+
+import concourse.mybir as mybir
+
+K, T, J, R, V, N, Z, E = 512, 2048, 256, 512, 512, 256, 1024, 128
+FLOPS = 2 * K * R * J * 2 + 2 * R * N * J * 2
+
+F32 = mybir.dt.float32
+BF16 = mybir.dt.bfloat16
+I32 = mybir.dt.int32
+U32 = mybir.dt.uint32
+U16 = mybir.dt.uint16
+U8 = mybir.dt.uint8
+E4M3 = mybir.dt.float8_e4m3fn_x4
+E5M2 = mybir.dt.float8_e5m2_x4
+E2M1 = mybir.dt.float4_e2m1fn_x4
+MULT = mybir.AluOpType.mult
+ADD = mybir.AluOpType.add
+COPY = mybir.ActivationFunctionType.Copy
+
+P = 128
+PACK = 4
+HALF = J // 2
+XT_COL, XO_COL, W_COL, WB_COL = 0, J, 2 * J, 2 * J + R
+PLANE_COLS = WB_COL + N
+
+
+def tile_list_firstorder_notes_changes_kernel(
+    tc, xt_words, xt_scales, w_words, w_scales, xo_words, xo_scales, tb, wb_words, wb_scales,
+    offs, offs2, offs3, offs4, offs5, offs6, out,
+):
+    nc = tc.nc
+    with ExitStack() as ctx:
+        keep = ctx.enter_context(tc.tile_pool(name="keep", bufs=1))
+        psum = ctx.enter_context(tc.psum_pool(name="psum", bufs=1))
+
+        def sb(name, shape, dtype):
+            return keep.tile(shape, dtype, name=name, align_bytes=64)
+
+        idx_xt = sb("idx_xt", [P, J // 16], U16)
+        idx_xo = sb("idx_xo", [P, J // 16], U16)
+        idx_t3 = sb("idx_t3", [P, J // 16], U16)
+        idx_t4 = sb("idx_t4", [P, J // 16], U16)
+        idx_p = sb("idx_p", [P, E // 16], U16)
+        idx_dp = sb("idx_dp", [P, E // 16], U16)
+
+        xt_rows = sb("xt_rows", [P, T], U8)
+        xo_rows = sb("xo_rows", [P, Z], U8)
+        w_rows = sb("w_rows", [P, R], U8)
+        planes = sb("planes", [P, PLANE_COLS], U8)
+        xt_all = sb("xt_all", [P, T], U32)
+        xo_all = sb("xo_all", [P, Z], U32)
+        w_raw = sb("w_raw", [P, 2 * R], U8)
+        w_codes = sb("w_codes", [P, 2 * R], U8)
+        wb_codes = sb("wb_codes", [P, 2 * N], U8)
+        tb_pair = [sb("tb_pair%d" % u, [P, 2, V], F32) for u in range(2)]
+
+        nc.vector.memset(xt_rows[:].bitcast(I32), 0)
+        nc.gpsimd.memset(w_rows[:].bitcast(I32), 0)
+        nc.gpsimd.memset(xo_rows[:].bitcast(I32), 0)
+        nc.vector.memset(planes[:, WB_COL:PLANE_COLS].bitcast(I32), 0)
+
+        tb_dealt = tb.rearrange("(p t) v -> p t v", t=PACK)
+        nc.scalar.dma_start(w_rows[0:P:8, :].bitcast(I32), w_scales[0].bitcast(I32))
+        nc.scalar.dma_start(xo_rows[0:P:8, :].bitcast(I32), xo_scales[0].bitcast(I32))
+        nc.scalar.dma_start(xt_rows[0:P:8, :].bitcast(I32), xt_scales[0].bitcast(I32))
+        nc.sync.dma_start(idx_xo[:], offs2)
+        nc.sync.dma_start(idx_xt[:], offs)
+        nc.sync.dma_start(idx_t3[:], offs3)
+        nc.sync.dma_start(tb_pair[0][:], tb_dealt[:, 0:2, :])
+        nc.sync.dma_start(tb_pair[1][:], tb_dealt[:, 2:4, :])
+        nc.sync.dma_start(planes[0:P:8, WB_COL:PLANE_COLS].bitcast(I32), wb_scales[0].bitcast(I32))
+        nc.sync.dma_start(w_raw[:].bitcast(I32), w_words[0].bitcast(I32))
+        nc.sync.dma_start(idx_t4[:], offs4)
+        nc.sync.dma_start(xo_all[:].bitcast(I32), xo_words[0].rearrange("p c b -> p (c b)").bitcast(I32))
+        nc.sync.dma_start(xt_all[:].bitcast(I32), xt_words[0].rearrange("p c b -> p (c b)").bitcast(I32))
+        nc.sync.dma_start(wb_codes[:].bitcast(I32), wb_words[0].bitcast(I32))
+        nc.sync.dma_start(idx_dp[:], offs6)
+        nc.sync.dma_start(idx_p[:], offs5)
+
+        xo_picked_rows = sb("xo_picked_rows", [P, J], U8)
+        xt_picked_rows = sb("xt_picked_rows", [P, J], U8)
+        nc.vector.tensor_copy(
+            planes[:, W_COL:WB_COL].rearrange("p (t m) -> p t m", t=PACK),
+            w_rows[:].rearrange("p (m t) -> p t m", t=PACK),
+        )
+        nc.vector.tensor_copy(xo_picked_rows[:], xo_rows[:].indirect(idx_xo[:]))
+        nc.vector.tensor_copy(xt_picked_rows[:], xt_rows[:].indirect(idx_xt[:]))
+        nc.vector.tensor_copy(planes[:, XO_COL:W_COL].bitcast(I32), xo_picked_rows[:].bitcast(I32))
+        nc.vector.tensor_copy(planes[:, XT_COL:XO_COL].bitcast(I32), xt_picked_rows[:].bitcast(I32))
+        for r in range(1, 4):
+            nc.scalar.dma_start(planes[r:P:32, :].bitcast(I32), planes[8 * r : P : 32, :].bitcast(I32))
+
+        nc.vector.tensor_copy(
+            w_codes[:].bitcast(U16).rearrange("p (t m) -> p t m", t=PACK),
+            w_raw[:].bitcast(U16).rearrange("p (m t) -> p t m", t=PACK),
+        )
+
+        t3 = sb("t3", [P, PACK, J], F32)
+        t4 = sb("t4", [P, PACK, J], F32)
+        for t in range(PACK):
+            nc.scalar.activation(t3[:, t, :], tb_pair[t // 2][:, t % 2, :].indirect(idx_t3[:]), COPY)
+        for t in range(PACK):
+            nc.scalar.activation(t4[:, t, :], tb_pair[t // 2][:, t % 2, :].indirect(idx_t4[:]), COPY)
+
+        def first_stage(dst, t, rhs, rhs_scale):
+            nc.tensor.matmul_mx(
+                out=dst,
+                lhsT=w_codes[:, 2 * P * t : 2 * P * (t + 1)].bitcast(E2M1),
+                lhsT_scale=planes[:, W_COL + P * t : W_COL + P * (t + 1)],
+                rhs=rhs, rhs_scale=rhs_scale, start=True, stop=True,
+            )
+
+        xo_picked = sb("xo_picked", [P, J], U32)
+        nc.vector.tensor_copy(xo_picked[:], xo_all[:].indirect(idx_xo[:]))
+        da = [psum.tile([P, 2, J], F32, name="da%d" % u, tag="da%d" % u) for u in range(2)]
+        m1 = sb("m1", [P, PACK, J], F32)
+        for t in range(PACK):
+            first_stage(da[t // 2][:, t % 2, :], t, xo_picked[:].bitcast(E4M3), planes[:, XO_COL : XO_COL + J])
+        for u in range(2):
+            nc.vector.tensor_tensor(m1[:, 2 * u : 2 * u + 2, :], da[u][:], t3[:, 2 * u : 2 * u + 2, :], MULT)
+
+        xt_picked = sb("xt_picked", [P, J], U32)
+        a = [psum.tile([P, PACK, HALF], F32, name="a%d" % s) for s in range(2)]
+        halves = [slice(s * HALF, (s + 1) * HALF) for s in range(2)]
+        for s in range(2):
+            nc.vector.tensor_copy(xt_picked[:, halves[s]], xt_all[:].indirect(idx_xt[:, 8 * s : 8 * (s + 1)]))
+            for t in range(PACK):
+                first_stage(a[s][:, t, :], t, xt_picked[:, halves[s]].bitcast(E5M2),
+                            planes[:, XT_COL + s * HALF : XT_COL + (s + 1) * HALF])
+
+        def planar(ap):
+            return ap.rearrange("p t (c i) -> p c t i", i=4)
+
+        def woven(ap):
+            return ap.rearrange("p (c i t) -> p c t i", i=4, t=PACK)
+
+        m2 = [sb("m2_%d" % s, [P, PACK, HALF], F32) for s in range(2)]
+        dh = [sb("dh%d" % s, [P, HALF * PACK], BF16) for s in range(2)]
+        hid = [sb("hid%d" % s, [P, HALF * PACK], BF16) for s in range(2)]
+        dh_codes = sb("dh_codes", [P, J], U32)
+        dh_plane = sb("dh_plane", [P, J], U8)
+        hid_codes = sb("hid_codes", [P, J], U32)
+        hid_plane = sb("hid_plane", [P, J], U8)
+
+        def second_stage(dst, h, rhs, rhs_scale):
+            nc.tensor.matmul_mx(
+                out=dst,
+                lhsT=wb_codes[:, 2 * P * h : 2 * P * (h + 1)].bitcast(E2M1),
+                lhsT_scale=planes[:, WB_COL + P * h : WB_COL + P * (h + 1)],
+                rhs=rhs, rhs_scale=rhs_scale, start=True, stop=True,
+            )
+
+        dp = [sb("dp%d" % h, [P, J], F32) for h in range(2)]
+        p = [sb("p%d" % h, [P, J], F32) for h in range(2)]
+        dp_picked = [sb("dp_picked%d" % h, [P, E], F32) for h in range(2)]
+        result = [sb("result%d" % h, [P, E], F32) for h in range(2)]
+
+        def dp_half(s):
+            nc.vector.quantize_mx(out=dh_codes[:, halves[s]].bitcast(E5M2), scales=dh_plane[:, halves[s]], in_=dh[s][:])
+            sums = psum.tile([P, 2, HALF], F32, name="dp_sum%d" % s)
+            for h in range(2):
+                second_stage(sums[:, h, :], h, dh_codes[:, halves[s]].bitcast(E5M2), dh_plane[:, halves[s]])
+            for h in range(2):
+                nc.scalar.copy(dp[h][:, halves[s]], sums[:, h, :])
+
+        def hid_half(s):
+            nc.vector.tensor_tensor(woven(hid[s][:]), planar(a[s][:]), planar(t3[:, :, halves[s]]), MULT)
+
+        for s in range(2):
+            nc.vector.tensor_tensor(m2[s][:], a[s][:], t4[:, :, halves[s]], MULT)
+        for s in range(2):
+            nc.vector.tensor_tensor(woven(dh[s][:]), planar(m1[:, :, halves[s]]), planar(m2[s][:]), ADD)
+        for s in range(2):
+            dp_half(s)
+            hid_half(s)
+        for h in range(2):
+            nc.scalar.activation(dp_picked[h][:], dp[h][:].indirect(idx_dp[:]), COPY, scale=-0.5)
+        p_sum = [[psum.tile([P, HALF], F32, name="p_sum%d%d" % (s, h), tag=("da%d" % h if s == 0 else "p%d" % h))
+                  for h in range(2)] for s in range(2)]
+        for s in range(2):
+            nc.vector.quantize_mx(out=hid_codes[:, halves[s]].bitcast(E4M3), scales=hid_plane[:, halves[s]], in_=hid[s][:])
+            for h in range(2):
+                second_stage(p_sum[s][h][:], h, hid_codes[:, halves[s]].bitcast(E4M3), hid_plane[:, halves[s]])
+        for h in range(2):
+            nc.vector.tensor_copy(p[h][:, halves[0]], p_sum[0][h][:])
+        nc.vector.tensor_copy(p[0][:, halves[1]], p_sum[1][0][:])
+        nc.scalar.copy(p[1][:, halves[1]], p_sum[1][1][:])
+        for h in range(2):
+            nc.vector.tensor_tensor(result[h][:], p[h][:].indirect(idx_p[:]), dp_picked[h][:], ADD)
+        nc.sync.dma_start(out[0:P, :], result[0][:])
+        nc.scalar.dma_start(out[P : 2 * P, :], result[1][:])

@@ -58,6 +58,9 @@ def tile_list_firstorder_notes_changes_kernel(
         nc.vector.memset(xt_rows[:].bitcast(I32), 0)
         nc.gpsimd.memset(w_rows[:].bitcast(I32), 0)
         nc.gpsimd.memset(xo_rows[:].bitcast(I32), 0)
+        warm = sb("warm", [P, 16], F32)
+        nc.gpsimd.memset(warm[:, 0:8], 0.0)
+        nc.scalar.activation(warm[:, 8:9], warm[:, 0:1], COPY)
         nc.vector.memset(planes[:, WB_COL:PLANE_COLS].bitcast(I32), 0)
 
         tb_dealt = tb.rearrange("(p t) v -> p t v", t=PACK)

@@ -49,41 +49,37 @@ def tile_list_firstorder_notes_changes_kernel(
         w_rows = sb("w_rows", [P, R], U8)
         planes = sb("planes", [P, PLANE_COLS], U8)
         xt_all = sb("xt_all", [P, T], U32)
-        xo_all = sb("xo_all", [P, Z], U32)
-        w_raw = sb("w_raw", [P, 2 * R], U8)
+        w_raw = keep.tile([P, 2 * R], U8, name="w_raw", tag="w_then_wb", align_bytes=64)
         w_codes = sb("w_codes", [P, 2 * R], U8)
-        wb_codes = sb("wb_codes", [P, 2 * N], U8)
         tb_pair = [sb("tb_pair%d" % u, [P, 2, V], F32) for u in range(2)]
 
-        nc.vector.memset(xt_rows[:].bitcast(I32), 0)
         nc.gpsimd.memset(w_rows[:].bitcast(I32), 0)
-        nc.gpsimd.memset(xo_rows[:].bitcast(I32), 0)
+        nc.vector.memset(xo_rows[:].bitcast(I32), 0)
+        nc.vector.memset(xt_rows[:].bitcast(I32), 0)
+        nc.gpsimd.memset(planes[:, WB_COL:PLANE_COLS].bitcast(I32), 0)
         warm = sb("warm", [P, 16], F32)
         nc.gpsimd.memset(warm[:, 0:8], 0.0)
         nc.scalar.activation(warm[:, 8:9], warm[:, 0:1], COPY)
-        nc.vector.memset(planes[:, WB_COL:PLANE_COLS].bitcast(I32), 0)
 
         tb_dealt = tb.rearrange("(p t) v -> p t v", t=PACK)
-        nc.scalar.dma_start(w_rows[0:P:8, :].bitcast(I32), w_scales[0].bitcast(I32))
-        nc.scalar.dma_start(xo_rows[0:P:8, :].bitcast(I32), xo_scales[0].bitcast(I32))
-        nc.scalar.dma_start(xt_rows[0:P:8, :].bitcast(I32), xt_scales[0].bitcast(I32))
-        nc.sync.dma_start(idx_xo[:], offs2)
+        nc.gpsimd.dma_start(planes[0:P:8, WB_COL:PLANE_COLS].bitcast(I32), wb_scales[0].bitcast(I32))
         nc.sync.dma_start(idx_xt[:], offs)
+        nc.sync.dma_start(idx_xo[:], offs2)
         nc.sync.dma_start(idx_t3[:], offs3)
+        nc.sync.dma_start(w_rows[0:P:8, :].bitcast(I32), w_scales[0].bitcast(I32))
+        nc.sync.dma_start(xo_rows[0:P:8, :].bitcast(I32), xo_scales[0].bitcast(I32))
+        nc.sync.dma_start(xt_rows[0:P:8, :].bitcast(I32), xt_scales[0].bitcast(I32))
         nc.sync.dma_start(tb_pair[0][:], tb_dealt[:, 0:2, :])
         nc.sync.dma_start(tb_pair[1][:], tb_dealt[:, 2:4, :])
-        nc.sync.dma_start(planes[0:P:8, WB_COL:PLANE_COLS].bitcast(I32), wb_scales[0].bitcast(I32))
         nc.sync.dma_start(w_raw[:].bitcast(I32), w_words[0].bitcast(I32))
         nc.sync.dma_start(idx_t4[:], offs4)
-        nc.sync.dma_start(xo_all[:].bitcast(I32), xo_words[0].rearrange("p c b -> p (c b)").bitcast(I32))
         nc.sync.dma_start(xt_all[:].bitcast(I32), xt_words[0].rearrange("p c b -> p (c b)").bitcast(I32))
-        nc.sync.dma_start(wb_codes[:].bitcast(I32), wb_words[0].bitcast(I32))
         nc.sync.dma_start(idx_dp[:], offs6)
         nc.sync.dma_start(idx_p[:], offs5)
 
         xo_picked_rows = sb("xo_picked_rows", [P, J], U8)
-        xt_picked_rows = sb("xt_picked_rows", [P, J], U8)
-        nc.vector.tensor_copy(
+        xt_picked_rows = keep.tile([P, J], U8, name="xt_picked_rows", tag="rows_then_xo", align_bytes=64)
+        nc.gpsimd.tensor_copy(
             planes[:, W_COL:WB_COL].rearrange("p (t m) -> p t m", t=PACK),
             w_rows[:].rearrange("p (m t) -> p t m", t=PACK),
         )
@@ -92,12 +88,17 @@ def tile_list_firstorder_notes_changes_kernel(
         nc.vector.tensor_copy(planes[:, XO_COL:W_COL].bitcast(I32), xo_picked_rows[:].bitcast(I32))
         nc.vector.tensor_copy(planes[:, XT_COL:XO_COL].bitcast(I32), xt_picked_rows[:].bitcast(I32))
         for r in range(1, 4):
-            nc.scalar.dma_start(planes[r:P:32, :].bitcast(I32), planes[8 * r : P : 32, :].bitcast(I32))
+            nc.sync.dma_start(planes[r:P:32, :].bitcast(I32), planes[8 * r : P : 32, :].bitcast(I32))
+        xo_all = keep.tile([P, Z], U32, name="xo_all", tag="rows_then_xo", align_bytes=64)
+        nc.sync.dma_start(xo_all[:].bitcast(I32), xo_words[0].rearrange("p c b -> p (c b)").bitcast(I32))
 
         nc.vector.tensor_copy(
             w_codes[:].bitcast(U16).rearrange("p (t m) -> p t m", t=PACK),
             w_raw[:].bitcast(U16).rearrange("p (m t) -> p t m", t=PACK),
         )
+
+        wb_codes = keep.tile([P, 2 * N], U8, name="wb_codes", tag="w_then_wb", align_bytes=64)
+        nc.sync.dma_start(wb_codes[:].bitcast(I32), wb_words[0].bitcast(I32))
 
         t3 = sb("t3", [P, PACK, J], F32)
         t4 = sb("t4", [P, PACK, J], F32)
@@ -114,38 +115,6 @@ def tile_list_firstorder_notes_changes_kernel(
                 rhs=rhs, rhs_scale=rhs_scale, start=True, stop=True,
             )
 
-        xo_picked = sb("xo_picked", [P, J], U32)
-        nc.vector.tensor_copy(xo_picked[:], xo_all[:].indirect(idx_xo[:]))
-        da = [psum.tile([P, 2, J], F32, name="da%d" % u, tag="da%d" % u) for u in range(2)]
-        m1 = sb("m1", [P, PACK, J], F32)
-        for t in range(PACK):
-            first_stage(da[t // 2][:, t % 2, :], t, xo_picked[:].bitcast(E4M3), planes[:, XO_COL : XO_COL + J])
-        for u in range(2):
-            nc.vector.tensor_tensor(m1[:, 2 * u : 2 * u + 2, :], da[u][:], t3[:, 2 * u : 2 * u + 2, :], MULT)
-
-        xt_picked = sb("xt_picked", [P, J], U32)
-        a = [psum.tile([P, PACK, HALF], F32, name="a%d" % s) for s in range(2)]
-        halves = [slice(s * HALF, (s + 1) * HALF) for s in range(2)]
-        for s in range(2):
-            nc.vector.tensor_copy(xt_picked[:, halves[s]], xt_all[:].indirect(idx_xt[:, 8 * s : 8 * (s + 1)]))
-            for t in range(PACK):
-                first_stage(a[s][:, t, :], t, xt_picked[:, halves[s]].bitcast(E5M2),
-                            planes[:, XT_COL + s * HALF : XT_COL + (s + 1) * HALF])
-
-        def planar(ap):
-            return ap.rearrange("p t (c i) -> p c t i", i=4)
-
-        def woven(ap):
-            return ap.rearrange("p (c i t) -> p c t i", i=4, t=PACK)
-
-        m2 = [sb("m2_%d" % s, [P, PACK, HALF], F32) for s in range(2)]
-        dh = [sb("dh%d" % s, [P, HALF * PACK], BF16) for s in range(2)]
-        hid = [sb("hid%d" % s, [P, HALF * PACK], BF16) for s in range(2)]
-        dh_codes = sb("dh_codes", [P, J], U32)
-        dh_plane = sb("dh_plane", [P, J], U8)
-        hid_codes = sb("hid_codes", [P, J], U32)
-        hid_plane = sb("hid_plane", [P, J], U8)
-
         def second_stage(dst, h, rhs, rhs_scale):
             nc.tensor.matmul_mx(
                 out=dst,
@@ -154,41 +123,79 @@ def tile_list_firstorder_notes_changes_kernel(
                 rhs=rhs, rhs_scale=rhs_scale, start=True, stop=True,
             )
 
+        def planar(ap):
+            return ap.rearrange("p t (c i) -> p c t i", i=4)
+
+        def woven(ap):
+            return ap.rearrange("p (c i t) -> p c t i", i=4, t=PACK)
+
+        halves = [slice(s * HALF, (s + 1) * HALF) for s in range(2)]
+        xt_picked = sb("xt_picked", [P, J], U32)
+        xo_picked = sb("xo_picked", [P, J], U32)
+        a = [psum.tile([P, PACK, HALF], F32, name="a%d" % s) for s in range(2)]
+        da = [psum.tile([P, PACK, HALF], F32, name="da%d" % s, tag="da%d" % s) for s in range(2)]
+        m1 = [sb("m1_%d" % s, [P, PACK, HALF], F32) for s in range(2)]
+        m2 = [sb("m2_%d" % s, [P, PACK, HALF], F32) for s in range(2)]
+        dh = [keep.tile([P, HALF * PACK], BF16, name="dh%d" % s, tag="dh%d" % s, align_bytes=64) for s in range(2)]
+        hid = [sb("hid0", [P, HALF * PACK], BF16)]
+        dh_codes = sb("dh_codes", [P, J], U32)
+        dh_plane = sb("dh_plane", [P, J], U8)
+        hid_codes = sb("hid_codes", [P, J], U32)
+        hid_plane = sb("hid_plane", [P, J], U8)
         dp = [sb("dp%d" % h, [P, J], F32) for h in range(2)]
         p = [sb("p%d" % h, [P, J], F32) for h in range(2)]
         dp_picked = [sb("dp_picked%d" % h, [P, E], F32) for h in range(2)]
         result = [sb("result%d" % h, [P, E], F32) for h in range(2)]
 
+        def hid_half(s):
+            nc.vector.tensor_tensor(woven(hid[s][:]), planar(a[s][:]), planar(t3[:, :, halves[s]]), MULT)
+
+        def quantise_hid(s):
+            nc.vector.quantize_mx(out=hid_codes[:, halves[s]].bitcast(E4M3), scales=hid_plane[:, halves[s]], in_=hid[s][:])
+
         def dp_half(s):
             nc.vector.quantize_mx(out=dh_codes[:, halves[s]].bitcast(E5M2), scales=dh_plane[:, halves[s]], in_=dh[s][:])
-            sums = psum.tile([P, 2, HALF], F32, name="dp_sum%d" % s)
+            sums = psum.tile([P, 2, HALF], F32, name="dp_sum%d" % s, tag="da%d" % s)
             for h in range(2):
                 second_stage(sums[:, h, :], h, dh_codes[:, halves[s]].bitcast(E5M2), dh_plane[:, halves[s]])
             for h in range(2):
                 nc.scalar.copy(dp[h][:, halves[s]], sums[:, h, :])
 
-        def hid_half(s):
-            nc.vector.tensor_tensor(woven(hid[s][:]), planar(a[s][:]), planar(t3[:, :, halves[s]]), MULT)
-
+        for s in range(2):
+            nc.vector.tensor_copy(xt_picked[:, halves[s]], xt_all[:].indirect(idx_xt[:, 8 * s : 8 * (s + 1)]))
+            for t in range(PACK):
+                first_stage(a[s][:, t, :], t, xt_picked[:, halves[s]].bitcast(E5M2),
+                            planes[:, XT_COL + s * HALF : XT_COL + (s + 1) * HALF])
+        hid_half(0)
+        nc.vector.tensor_copy(xo_picked[:], xo_all[:].indirect(idx_xo[:]))
+        for s in range(2):
+            for t in range(PACK):
+                first_stage(da[s][:, t, :], t, xo_picked[:, halves[s]].bitcast(E4M3),
+                            planes[:, XO_COL + s * HALF : XO_COL + (s + 1) * HALF])
+        quantise_hid(0)
+        p_first = psum.tile([P, 2, HALF], F32, name="p_first")
+        for h in range(2):
+            second_stage(p_first[:, h, :], h, hid_codes[:, halves[0]].bitcast(E4M3), hid_plane[:, halves[0]])
+        for h in range(2):
+            nc.scalar.copy(p[h][:, halves[0]], p_first[:, h, :])
         for s in range(2):
             nc.vector.tensor_tensor(m2[s][:], a[s][:], t4[:, :, halves[s]], MULT)
         for s in range(2):
-            nc.vector.tensor_tensor(woven(dh[s][:]), planar(m1[:, :, halves[s]]), planar(m2[s][:]), ADD)
+            nc.vector.tensor_tensor(m1[s][:], da[s][:], t3[:, :, halves[s]], MULT)
+        for s in range(2):
+            nc.vector.tensor_tensor(woven(dh[s][:]), planar(m1[s][:]), planar(m2[s][:]), ADD)
         for s in range(2):
             dp_half(s)
-            hid_half(s)
         for h in range(2):
             nc.scalar.activation(dp_picked[h][:], dp[h][:].indirect(idx_dp[:]), COPY, scale=-0.5)
-        p_sum = [[psum.tile([P, HALF], F32, name="p_sum%d%d" % (s, h), tag=("da%d" % h if s == 0 else "p%d" % h))
-                  for h in range(2)] for s in range(2)]
-        for s in range(2):
-            nc.vector.quantize_mx(out=hid_codes[:, halves[s]].bitcast(E4M3), scales=hid_plane[:, halves[s]], in_=hid[s][:])
-            for h in range(2):
-                second_stage(p_sum[s][h][:], h, hid_codes[:, halves[s]].bitcast(E4M3), hid_plane[:, halves[s]])
+        hid.append(keep.tile([P, HALF * PACK], BF16, name="hid1", tag="dh0", align_bytes=64))
+        hid_half(1)
+        quantise_hid(1)
+        p_last = [psum.tile([P, HALF], F32, name="p_last%d" % h) for h in range(2)]
         for h in range(2):
-            nc.vector.tensor_copy(p[h][:, halves[0]], p_sum[0][h][:])
-        nc.vector.tensor_copy(p[0][:, halves[1]], p_sum[1][0][:])
-        nc.scalar.copy(p[1][:, halves[1]], p_sum[1][1][:])
+            second_stage(p_last[h][:], h, hid_codes[:, halves[1]].bitcast(E4M3), hid_plane[:, halves[1]])
+        nc.vector.tensor_copy(p[0][:, halves[1]], p_last[0][:])
+        nc.scalar.copy(p[1][:, halves[1]], p_last[1][:])
         for h in range(2):
             nc.vector.tensor_tensor(result[h][:], p[h][:].indirect(idx_p[:]), dp_picked[h][:], ADD)
         nc.sync.dma_start(out[0:P, :], result[0][:])

@@ -66,10 +66,10 @@ def tile_list_firstorder_notes_changes_kernel(
         nc.sync.dma_start(idx_xt[:], offs)
         nc.sync.dma_start(idx_xo[:], offs2)
         nc.sync.dma_start(idx_t3[:], offs3)
+        nc.sync.dma_start(tb_pair[0][:], tb_dealt[:, 0:2, :])
         nc.sync.dma_start(w_rows[0:P:8, :].bitcast(I32), w_scales[0].bitcast(I32))
         nc.sync.dma_start(xo_rows[0:P:8, :].bitcast(I32), xo_scales[0].bitcast(I32))
         nc.sync.dma_start(xt_rows[0:P:8, :].bitcast(I32), xt_scales[0].bitcast(I32))
-        nc.sync.dma_start(tb_pair[0][:], tb_dealt[:, 0:2, :])
         nc.sync.dma_start(tb_pair[1][:], tb_dealt[:, 2:4, :])
         nc.sync.dma_start(w_raw[:].bitcast(I32), w_words[0].bitcast(I32))
         nc.sync.dma_start(idx_t4[:], offs4)
@@ -135,7 +135,7 @@ def tile_list_firstorder_notes_changes_kernel(
         a = [psum.tile([P, PACK, HALF], F32, name="a%d" % s) for s in range(2)]
         da = [psum.tile([P, PACK, HALF], F32, name="da%d" % s, tag="da%d" % s) for s in range(2)]
         m1 = [sb("m1_%d" % s, [P, PACK, HALF], F32) for s in range(2)]
-        m2 = [sb("m2_%d" % s, [P, PACK, HALF], F32) for s in range(2)]
+        m2 = [sb("m2_0", [P, PACK, HALF], F32)]
         dh = [keep.tile([P, HALF * PACK], BF16, name="dh%d" % s, tag="dh%d" % s, align_bytes=64) for s in range(2)]
         hid = [sb("hid0", [P, HALF * PACK], BF16)]
         dh_codes = sb("dh_codes", [P, J], U32)
@@ -167,8 +167,9 @@ def tile_list_firstorder_notes_changes_kernel(
                 first_stage(a[s][:, t, :], t, xt_picked[:, halves[s]].bitcast(E5M2),
                             planes[:, XT_COL + s * HALF : XT_COL + (s + 1) * HALF])
         hid_half(0)
-        nc.vector.tensor_copy(xo_picked[:], xo_all[:].indirect(idx_xo[:]))
+        nc.vector.tensor_tensor(m2[0][:], a[0][:], t4[:, :, halves[0]], MULT)
         for s in range(2):
+            nc.vector.tensor_copy(xo_picked[:, halves[s]], xo_all[:].indirect(idx_xo[:, 8 * s : 8 * (s + 1)]))
             for t in range(PACK):
                 first_stage(da[s][:, t, :], t, xo_picked[:, halves[s]].bitcast(E4M3),
                             planes[:, XO_COL + s * HALF : XO_COL + (s + 1) * HALF])
@@ -178,8 +179,8 @@ def tile_list_firstorder_notes_changes_kernel(
             second_stage(p_first[:, h, :], h, hid_codes[:, halves[0]].bitcast(E4M3), hid_plane[:, halves[0]])
         for h in range(2):
             nc.scalar.copy(p[h][:, halves[0]], p_first[:, h, :])
-        for s in range(2):
-            nc.vector.tensor_tensor(m2[s][:], a[s][:], t4[:, :, halves[s]], MULT)
+        m2.append(keep.tile([P, PACK, HALF], F32, name="m2_1", tag="rows_then_xo", align_bytes=64))
+        nc.vector.tensor_tensor(m2[1][:], a[1][:], t4[:, :, halves[1]], MULT)
         for s in range(2):
             nc.vector.tensor_tensor(m1[s][:], da[s][:], t3[:, :, halves[s]], MULT)
         for s in range(2):

from contextlib import ExitStack

import concourse.mybir as mybir

K, T, J, R, V, N, Z, E = 512, 2048, 256, 512, 512, 256, 1024, 128
FLOPS = 2 * K * R * J * 2 + 2 * R * N * J * 2

F32 = mybir.dt.float32
BF16 = mybir.dt.bfloat16
I32 = mybir.dt.int32
U32 = mybir.dt.uint32
U16 = mybir.dt.uint16
U8 = mybir.dt.uint8
E4M3 = mybir.dt.float8_e4m3fn_x4
E5M2 = mybir.dt.float8_e5m2_x4
E2M1 = mybir.dt.float4_e2m1fn_x4
MULT = mybir.AluOpType.mult
ADD = mybir.AluOpType.add
COPY = mybir.ActivationFunctionType.Copy

P = 128
PACK = 4
HALF = J // 2
XT_COL, XO_COL, W_COL, WB_COL = 0, J, 2 * J, 2 * J + R
PLANE_COLS = WB_COL + N


def tile_list_firstorder_notes_changes_kernel(
    tc, xt_words, xt_scales, w_words, w_scales, xo_words, xo_scales, tb, wb_words, wb_scales,
    offs, offs2, offs3, offs4, offs5, offs6, out,
):
    nc = tc.nc
    with ExitStack() as ctx:
        keep = ctx.enter_context(tc.tile_pool(name="keep", bufs=1))
        psum = ctx.enter_context(tc.psum_pool(name="psum", bufs=1))

        def sb(name, shape, dtype):
            return keep.tile(shape, dtype, name=name, align_bytes=64)

        idx_xt = sb("idx_xt", [P, J // 16], U16)
        idx_xo = sb("idx_xo", [P, J // 16], U16)
        idx_t3 = sb("idx_t3", [P, J // 16], U16)
        idx_t4 = sb("idx_t4", [P, J // 16], U16)
        idx_p = sb("idx_p", [P, E // 16], U16)
        idx_dp = sb("idx_dp", [P, E // 16], U16)

        xt_rows = sb("xt_rows", [P, T], U8)
        xo_rows = sb("xo_rows", [P, Z], U8)
        w_rows = sb("w_rows", [P, R], U8)
        planes = sb("planes", [P, PLANE_COLS], U8)
        xt_all = sb("xt_all", [P, T], U32)
        w_raw = keep.tile([P, 2 * R], U8, name="w_raw", tag="w_then_wb", align_bytes=64)
        w_codes = sb("w_codes", [P, 2 * R], U8)
        tb_pair = [sb("tb_pair%d" % u, [P, 2, V], F32) for u in range(2)]

        nc.gpsimd.memset(w_rows[:].bitcast(I32), 0)
        nc.vector.memset(xo_rows[:].bitcast(I32), 0)
        nc.vector.memset(xt_rows[:].bitcast(I32), 0)
        nc.gpsimd.memset(planes[:, WB_COL:PLANE_COLS].bitcast(I32), 0)
        warm = sb("warm", [P, 16], F32)
        nc.gpsimd.memset(warm[:, 0:8], 0.0)
        nc.scalar.activation(warm[:, 8:9], warm[:, 0:1], COPY)

        tb_dealt = tb.rearrange("(p t) v -> p t v", t=PACK)
        nc.gpsimd.dma_start(planes[0:P:8, WB_COL:PLANE_COLS].bitcast(I32), wb_scales[0].bitcast(I32))
        nc.sync.dma_start(idx_xt[:], offs)
        nc.sync.dma_start(idx_xo[:], offs2)
        nc.sync.dma_start(idx_t3[:], offs3)
        nc.sync.dma_start(tb_pair[0][:], tb_dealt[:, 0:2, :])
        nc.sync.dma_start(w_rows[0:P:8, :].bitcast(I32), w_scales[0].bitcast(I32))
        nc.sync.dma_start(xo_rows[0:P:8, :].bitcast(I32), xo_scales[0].bitcast(I32))
        nc.sync.dma_start(xt_rows[0:P:8, :].bitcast(I32), xt_scales[0].bitcast(I32))
        nc.sync.dma_start(tb_pair[1][:], tb_dealt[:, 2:4, :])
        nc.sync.dma_start(w_raw[:].bitcast(I32), w_words[0].bitcast(I32))
        nc.sync.dma_start(idx_t4[:], offs4)
        nc.sync.dma_start(xt_all[:].bitcast(I32), xt_words[0].rearrange("p c b -> p (c b)").bitcast(I32))
        nc.sync.dma_start(idx_dp[:], offs6)
        nc.sync.dma_start(idx_p[:], offs5)

        xo_picked_rows = sb("xo_picked_rows", [P, J], U8)
        xt_picked_rows = keep.tile([P, J], U8, name="xt_picked_rows", tag="rows_then_xo", align_bytes=64)
        nc.gpsimd.tensor_copy(
            planes[:, W_COL:WB_COL].rearrange("p (t m) -> p t m", t=PACK),
            w_rows[:].rearrange("p (m t) -> p t m", t=PACK),
        )
        nc.vector.tensor_copy(xo_picked_rows[:], xo_rows[:].indirect(idx_xo[:]))
        nc.vector.tensor_copy(xt_picked_rows[:], xt_rows[:].indirect(idx_xt[:]))
        nc.vector.tensor_copy(planes[:, XO_COL:W_COL].bitcast(I32), xo_picked_rows[:].bitcast(I32))
        nc.vector.tensor_copy(planes[:, XT_COL:XO_COL].bitcast(I32), xt_picked_rows[:].bitcast(I32))
        for r in range(1, 4):
            nc.sync.dma_start(planes[r:P:32, :].bitcast(I32), planes[8 * r : P : 32, :].bitcast(I32))
        xo_all = keep.tile([P, Z], U32, name="xo_all", tag="rows_then_xo", align_bytes=64)
        nc.sync.dma_start(xo_all[:].bitcast(I32), xo_words[0].rearrange("p c b -> p (c b)").bitcast(I32))

        nc.vector.tensor_copy(
            w_codes[:].bitcast(U16).rearrange("p (t m) -> p t m", t=PACK),
            w_raw[:].bitcast(U16).rearrange("p (m t) -> p t m", t=PACK),
        )

        wb_codes = keep.tile([P, 2 * N], U8, name="wb_codes", tag="w_then_wb", align_bytes=64)
        nc.sync.dma_start(wb_codes[:].bitcast(I32), wb_words[0].bitcast(I32))

        t3 = sb("t3", [P, PACK, J], F32)
        t4 = sb("t4", [P, PACK, J], F32)
        for t in range(PACK):
            nc.scalar.activation(t3[:, t, :], tb_pair[t // 2][:, t % 2, :].indirect(idx_t3[:]), COPY)
        for t in range(PACK):
            nc.scalar.activation(t4[:, t, :], tb_pair[t // 2][:, t % 2, :].indirect(idx_t4[:]), COPY)

        def first_stage(dst, t, rhs, rhs_scale):
            nc.tensor.matmul_mx(
                out=dst,
                lhsT=w_codes[:, 2 * P * t : 2 * P * (t + 1)].bitcast(E2M1),
                lhsT_scale=planes[:, W_COL + P * t : W_COL + P * (t + 1)],
                rhs=rhs, rhs_scale=rhs_scale, start=True, stop=True,
            )

        def second_stage(dst, h, rhs, rhs_scale):
            nc.tensor.matmul_mx(
                out=dst,
                lhsT=wb_codes[:, 2 * P * h : 2 * P * (h + 1)].bitcast(E2M1),
                lhsT_scale=planes[:, WB_COL + P * h : WB_COL + P * (h + 1)],
                rhs=rhs, rhs_scale=rhs_scale, start=True, stop=True,
            )

        def planar(ap):
            return ap.rearrange("p t (c i) -> p c t i", i=4)

        def woven(ap):
            return ap.rearrange("p (c i t) -> p c t i", i=4, t=PACK)

        halves = [slice(s * HALF, (s + 1) * HALF) for s in range(2)]
        xt_picked = sb("xt_picked", [P, J], U32)
        xo_picked = sb("xo_picked", [P, J], U32)
        a = [psum.tile([P, PACK, HALF], F32, name="a%d" % s) for s in range(2)]
        da = [psum.tile([P, PACK, HALF], F32, name="da%d" % s, tag="da%d" % s) for s in range(2)]
        m1 = [sb("m1_%d" % s, [P, PACK, HALF], F32) for s in range(2)]
        m2 = [sb("m2_0", [P, PACK, HALF], F32)]
        dh = [keep.tile([P, HALF * PACK], BF16, name="dh%d" % s, tag="dh%d" % s, align_bytes=64) for s in range(2)]
        hid = [sb("hid0", [P, HALF * PACK], BF16)]
        dh_codes = sb("dh_codes", [P, J], U32)
        dh_plane = sb("dh_plane", [P, J], U8)
        hid_codes = sb("hid_codes", [P, J], U32)
        hid_plane = sb("hid_plane", [P, J], U8)
        dp = [sb("dp%d" % h, [P, J], F32) for h in range(2)]
        p = [sb("p%d" % h, [P, J], F32) for h in range(2)]
        dp_picked = [sb("dp_picked%d" % h, [P, E], F32) for h in range(2)]
        result = [sb("result%d" % h, [P, E], F32) for h in range(2)]

        def hid_half(s):
            nc.vector.tensor_tensor(woven(hid[s][:]), planar(a[s][:]), planar(t3[:, :, halves[s]]), MULT)

        def quantise_hid(s):
            nc.vector.quantize_mx(out=hid_codes[:, halves[s]].bitcast(E4M3), scales=hid_plane[:, halves[s]], in_=hid[s][:])

        def dp_half(s):
            nc.vector.quantize_mx(out=dh_codes[:, halves[s]].bitcast(E5M2), scales=dh_plane[:, halves[s]], in_=dh[s][:])
            sums = psum.tile([P, 2, HALF], F32, name="dp_sum%d" % s, tag="da%d" % s)
            for h in range(2):
                second_stage(sums[:, h, :], h, dh_codes[:, halves[s]].bitcast(E5M2), dh_plane[:, halves[s]])
            for h in range(2):
                nc.scalar.copy(dp[h][:, halves[s]], sums[:, h, :])

        for s in range(2):
            nc.vector.tensor_copy(xt_picked[:, halves[s]], xt_all[:].indirect(idx_xt[:, 8 * s : 8 * (s + 1)]))
            for t in range(PACK):
                first_stage(a[s][:, t, :], t, xt_picked[:, halves[s]].bitcast(E5M2),
                            planes[:, XT_COL + s * HALF : XT_COL + (s + 1) * HALF])
        hid_half(0)
        nc.vector.tensor_tensor(m2[0][:], a[0][:], t4[:, :, halves[0]], MULT)
        for s in range(2):
            nc.vector.tensor_copy(xo_picked[:, halves[s]], xo_all[:].indirect(idx_xo[:, 8 * s : 8 * (s + 1)]))
            for t in range(PACK):
                first_stage(da[s][:, t, :], t, xo_picked[:, halves[s]].bitcast(E4M3),
                            planes[:, XO_COL + s * HALF : XO_COL + (s + 1) * HALF])
        quantise_hid(0)
        p_first = psum.tile([P, 2, HALF], F32, name="p_first")
        for h in range(2):
            second_stage(p_first[:, h, :], h, hid_codes[:, halves[0]].bitcast(E4M3), hid_plane[:, halves[0]])
        for h in range(2):
            nc.scalar.copy(p[h][:, halves[0]], p_first[:, h, :])
        m2.append(keep.tile([P, PACK, HALF], F32, name="m2_1", tag="rows_then_xo", align_bytes=64))
        nc.vector.tensor_tensor(m2[1][:], a[1][:], t4[:, :, halves[1]], MULT)
        for s in range(2):
            nc.vector.tensor_tensor(m1[s][:], da[s][:], t3[:, :, halves[s]], MULT)
        for s in range(2):
            nc.vector.tensor_tensor(woven(dh[s][:]), planar(m1[s][:]), planar(m2[s][:]), ADD)
        for s in range(2):
            dp_half(s)
        for h in range(2):
            nc.scalar.activation(dp_picked[h][:], dp[h][:].indirect(idx_dp[:]), COPY, scale=-0.5)
        hid.append(keep.tile([P, HALF * PACK], BF16, name="hid1", tag="dh0", align_bytes=64))
        hid_half(1)
        quantise_hid(1)
        p_last = [psum.tile([P, HALF], F32, name="p_last%d" % h) for h in range(2)]
        for h in range(2):
            second_stage(p_last[h][:], h, hid_codes[:, halves[1]].bitcast(E4M3), hid_plane[:, halves[1]])
        nc.vector.tensor_copy(p[0][:, halves[1]], p_last[0][:])
        nc.scalar.copy(p[1][:, halves[1]], p_last[1][:])
        for h in range(2):
            nc.vector.tensor_tensor(result[h][:], p[h][:].indirect(idx_p[:]), dp_picked[h][:], ADD)
        nc.sync.dma_start(out[0:P, :], result[0][:])
        nc.scalar.dma_start(out[P : 2 * P, :], result[1][:])
